import numpy as np, ml_dtypes
CORES = [2,3,42,43,82,83,122,123]
N = 8
import mx_ref
BF = ml_dtypes.bfloat16
def entries(a):
    return np.ascontiguousarray(a.T).reshape(-1)
def table(e):
    return np.ascontiguousarray(np.reshape(e, (-1, 16)).T).astype(np.int32)
def f(rng, *shape):
    return mx_ref.flush((rng.standard_normal(shape, dtype=np.float32) * np.exp2(rng.integers(-2, 3, shape[:-1] + (1,)))).astype(BF))
def wide(rng, *shape, cols=0):
    v = rng.standard_normal(shape, dtype=np.float32) * np.exp2(rng.integers(-12, 13, shape)).astype(np.float32)
    if cols: v *= np.repeat(np.exp2(rng.integers(-cols, cols + 1, shape[:-2] + (1, shape[-1] // 4))) * (rng.random(shape[:-2] + (1, shape[-1] // 4)) > 0.0625), 4, axis=-1).astype(np.float32)
    return mx_ref.flush(v.astype(BF))
T = 1024
def listed(a):
    k = np.full((2 * N, 128), -1)
    for s in range(2 * N):
        i = np.flatnonzero(a == s); k[s, :len(i)] = i
    return k.reshape(-1)
def lists(rng, one=False, absent=False, sort=False, alike=False):
    t, a, k = [], [], []; nobody = rng.integers(0, N)
    for r in range(N):
        if r == 0 or not alike:
            u = np.concatenate([rng.permutation(8)[:2] for q in range(N)])
            if absent:
                here = rng.permutation([q for q in range(N) if q != nobody])[:T // 256 + r % 3].tolist()
                u.reshape(N, 2)[[q for q in range(N) if q not in here]] = -1
            else: u[rng.permutation(2 * N)[:rng.integers(0, 5)]] = -1
        v = rng.permutation(np.flatnonzero(u >= 0))
        if one: e = np.concatenate([np.full(128, v[0]), np.resize(v[1:], T - 128)])
        else:
            room = np.zeros(2 * N, int); room[v] = rng.integers(0, 129, len(v))
            for s in v:
                if room.sum() < T: room[s] = 128
            e = np.repeat(np.arange(2 * N), room)
        e = rng.permutation(e)[:T]
        if sort: e = np.sort(e)
        t.append(table(u)); a.append(table(e)); k.append(table(listed(e)))
    return {"tab": np.stack(t), "ad": np.stack(a), "tok": np.stack(k)}
def setup_inputs(rng):
    return {"x": f(rng, N, 128, 4 * T), "wa": f(rng, N, 1024, 512), **lists(rng)}
def setup_inputs_absent(rng):
    return {**setup_inputs(rng), **lists(rng, absent=True)}
def setup_inputs_alike(rng):
    return {**setup_inputs(rng), **lists(rng, alike=True)}
def setup_inputs_one(rng):
    return {**setup_inputs(rng), **lists(rng, one=True)}
def setup_inputs_sorted(rng):
    return {**setup_inputs(rng), **lists(rng, sort=True)}
def setup_inputs_spread(rng):
    d = setup_inputs(rng); d["x"] = wide(rng, N, 128, 4 * T, cols=8); return d
def check_inputs(d):
    b = []
    for n in ("x", "wa"):
        v = np.abs(np.asarray(d[n]).astype(np.float32))
        if not ((v == 0) | ((v >= 2.0 ** -30) & (v <= 2.0 ** 30))).all(): b.append(n)
    for r in range(N):
        u, a, k = entries(d["tab"][r]), entries(d["ad"][r]), entries(d["tok"][r]); p = u.reshape(N, 2)
        if u.min() < -1 or u.max() > 7 or ((p[:, 0] == p[:, 1]) & (p[:, 0] >= 0)).any(): b.append("tab")
        if a.min() < 0 or a.max() >= 2 * N or (u[a] < 0).any() or np.bincount(a).max() > 128: b.append("ad")
        elif (k != listed(a)).any(): b.append("tok")
    return b
def reference(x, wa, tab, ad, tok):
    y = np.zeros((N, 128, T), np.float32)
    for r in range(N):
        u, a, X = entries(tab[r]), entries(ad[r]), mx_ref.quantize(x[r])
        for s in range(2 * N):
            i = np.flatnonzero(a == s)
            if len(i) == 0: continue
            A = wa[s // 2][128 * u[s]:128 * u[s] + 128]
            y[r][:, i] = mx_ref.matmul(mx_ref.quantize(A), X)[:, i]
    return {"y": y}

@@ -1,0 +1,375 @@
+from concourse.bass import DstId, RemoteDMATransfer, IndirectOffsetOnAxis
+from concourse.mybir import dt, AluOpType, ActivationFunctionType
+
+U8 = dt.uint8
+ADD, MUL, MAX, AND = AluOpType.add, AluOpType.mult, AluOpType.max, AluOpType.bitwise_and
+COPY = ActivationFunctionType.Copy
+
+F8 = "float8_e4m3fn_x4"
+I16 = ("sbuf", [128, 16], "int32")
+I2 = ("sbuf", [128, 2], "int32")
+SCRATCH = {
+    "tabd": ("dram", [128, 1], "int32"), "tabl": ("dram", [7, 128, 1], "int32"), "rtab": ("dram", [128, 1], "int32"),
+    "tv1": ("sbuf", [128, 12], "int32"), "tb1": ("sbuf", [128, 12], "int32"), "mf1": ("sbuf", [128, 12], "float32"),
+    "tv2": I2, "tb2": I2, "mf2": ("sbuf", [128, 2], "float32"), "tv3": I2, "tb3": I2, "mi3": I2, "ix3": I2,
+    "ibp": ("sbuf", [128, 32], "int32"), "ibc": ("sbuf", [128, 32], "int32"), "ibr": ("sbuf", [128, 32], "int32"),
+    "base": ("sbuf", [128, 32], "float32"), "offu": ("sbuf", [128, 448], "uint16"),
+    "tokb": ("sbuf", [128, 128], "int32"), "xo": ("sbuf", [128, 128], "uint16"),
+    "tk2": I16, "ka": I16, "kb": I16, "km": I16, "ka2": I16, "kmu": I16, "kc": I16, "kd": I16, "ut": I16,
+    "so": ("sbuf", [128, 16], "uint16"), "vals": ("sbuf", [128, 256], "float32"), "inv": ("sbuf", [128, 1392], "float32"),
+    "e2": ("dram", [16, 8, 64], "float32"), "mg": ("sbuf", [128, 512], "float32"), "s1": ("sbuf", [128, 256], "float32"),
+    "s2": ("sbuf", [128, 128], "float32"), "s3": ("sbuf", [128, 64], "float32"), "yo": ("sbuf", [128, 64], "uint16"),
+    "wab": ("sbuf", [128, 4096], "bfloat16"), "xsb": ("sbuf", [128, 4096], "bfloat16"), "hx": ("sbuf", [128, 8192], "bfloat16"),
+    "xq": ("sbuf", [128, 2048], F8), "xp": ("sbuf", [128, 2048], "uint8"),
+    "ga": ("sbuf", [128, 7168], "bfloat16"), "go": ("sbuf", [128, 1024], "bfloat16"),
+    "aq": ("sbuf", [128, 1792], F8), "apl": ("sbuf", [128, 1792], "uint8"),
+    "lc": ("sbuf", [128, 2048], F8), "lp": ("sbuf", [128, 2048], "uint8"),
+    "rlc": ("sbuf", [128, 768], F8), "rlp": ("sbuf", [128, 768], "uint8"),
+    "rsb": ("sbuf", [128, 2048], "float32"), "ysb": ("sbuf", [128, 1024], "float32"),
+    "ps": ("psum", [128, 4096], "float32"),
+}
+SEMAPHORES = (["d_tab", "d_own", "d_x", "d_tok", "d_tk2", "d_wa", "d_e1", "d_e2", "d_r1", "d_r2", "d_y", "d_go",
+               "v", "s", "p", "gq", "sent", "m_list", "m_nl", "rl"]
+              + ["rc%d" % k for k in range(3)] + ["rs%d" % k for k in range(3)] + ["arr%d" % q for q in range(8)])
+
+
+def bits(engines):
+    return sum(1 << e for e in engines)
+
+
+def layout(T, topo):
+    chips = []
+    for c in T.cores:
+        if topo.chip(c) not in chips:
+            chips.append(topo.chip(c))
+    ranks = [[r for r, c in enumerate(T.cores) if topo.chip(c) == ch] for ch in chips]
+    steps = sorted(range(1, len(chips)), key=lambda o: topo.same_plane(chips[0], chips[o]))
+    return chips, ranks, steps
+
+
+def relay_of(T, topo, core, place):
+    c = [k for k in topo.cores_of(core) if topo.die(k) != topo.die(core) and T.rank_of(k) is None
+         and all(topo.may_write(k, d) for d in T.cores)]
+    return c[place]
+
+
+def served(ranks, steps, h, i):
+    n = len(ranks)
+    return [ranks[(h + o) % n][1 - i] for o in steps], [ranks[(h + o) % n][i] for o in steps]
+
+
+def in_order(rl, dr):
+    return [rl[0], rl[1], dr[0], rl[2], dr[1], dr[2]]
+
+
+def relay_program(g, core, T, topo):
+    chips, ranks, steps = layout(T, topo)
+    if topo.chip(core) not in chips:
+        return
+    h = chips.index(topo.chip(core))
+    for i, r in enumerate(ranks[h]):
+        if relay_of(T, topo, T.cores[r], i) != core:
+            continue
+        me = T.sem
+        nb = T.cores[ranks[h][1 - i]]
+        dests = [T.cores[q] for q in served(ranks, steps, h, i)[0]]
+        eng = topo.engines(core, dests[0])
+        on = topo.engines(T.cores[r], core)
+        inner = [e for e in on if e not in topo.engines(T.cores[r], dests[0])]
+        a, b = 256 * r, 256 * r + 256
+        arr = me["arr%d" % r]
+        g.wait_ge(me.rl, len(on))
+        rid, pid, _ = topo.addr(nb)
+        g.remote_dma(T.tabl[6], T.rtab[:], me.m_nl, me.sent, pid, rid, bits(eng))
+        for k, d in enumerate(dests):
+            rid, pid, _ = topo.addr(d)
+            ins = len(inner if k else on)
+            g.wait_ge(me["rc%d" % k], ins)
+            g.remote_dma(T.lc[:, a:b].bitcast(U8), T.rlc[:, 256 * k:256 * k + 256].bitcast(U8), arr, me.sent, pid, rid, bits(eng))
+            g.wait_ge(me["rs%d" % k], ins)
+            g.remote_dma(T.lp[:, a:b], T.rlp[:, 256 * k:256 * k + 256], arr, me.sent, pid, rid, bits(eng))
+        g.wait_ge(me.sent, 7 * len(eng))
+
+
+def rank_program(g, core, T, topo):
+    rank = T.rank_of(core)
+    if rank is None:
+        return relay_program(g, core, T, topo)
+    chips, ranks, steps = layout(T, topo)
+    C = len(chips)
+    h = chips.index(topo.chip(core))
+    i = ranks[h].index(rank)
+    nbr = ranks[h][1 - i]
+    relay = relay_of(T, topo, core, i)
+    relayed, direct = served(ranks, steps, h, i)
+    out = in_order(relayed, direct)
+    rsrc = [ranks[(h - o) % C][1 - i] for o in steps]
+    dsrc = [ranks[(h - o) % C][i] for o in steps]
+    on = topo.engines(core, relay)
+    off = topo.engines(core, T.cores[out[0]])
+    inner = [e for e in on if e not in off]
+    S, V, P, Y = g.scalar, g.vector, g.tensor, g.sync
+    m = T.sem
+    cnt = {"v": 0, "s": 0, "p": 0, "gq": 0, "sent": 0}
+
+    def did(ins, name):
+        ins.then_inc(m[name], 1)
+        cnt[name] += 1
+        return cnt[name]
+
+    def v(ins): return did(ins, "v")
+    def s(ins): return did(ins, "s")
+    def gq(ins): return did(ins, "gq")
+
+    def dst_id(c):
+        rid, pid, _ = topo.addr(c)
+        return DstId(rid=rid, pnc=pid)
+
+    def place(q):
+        hq = [k for k in range(C) if q in ranks[k]][0]
+        return in_order(*served(ranks, steps, hq, ranks[hq].index(q))).index(rank)
+
+    def tok_loads(eng, ks):
+        for k in ks:
+            eng.dma_start(T.tk2[16 * k:16 * k + 16, :], T.tok[:, 16 * k:16 * k + 16]).then_inc(m.d_tk2, 16)
+        for k in ks:
+            eng.dma_start(T.tokb[16 * k:16 * k + 16, :], T.tok[:]).then_inc(m.d_tok, 16)
+
+    Y.dma_start(T.tabd[0:16, :], T.tab[:]).then_inc(m.d_tab, 16)
+    Y.dma_start(T.tabd[16:128, :], T.tok[0:1, 0:112]).then_inc(m.d_tab, 16)
+    S.dma_start(T.tv3[0:1, :], T.tab[2 * rank:2 * rank + 2, :]).then_inc(m.d_own, 16)
+    tok_loads(Y, range(0, 4))
+    tok_loads(S, range(4, 8))
+    Y.dma_start(T.xsb[:], T.x[:]).then_inc(m.d_x, 16)
+    gq(g.iota(T.ut[:], [[16, 16]], 65, 1))
+    gq(g.iota(T.ibp[:], [[0, 32]], 0, 1))
+    gq(g.iota(T.ibc[:], [[16, 32]], 0, 0))
+    g_b = gq(g.iota(T.vals[:], [[1, 256]], 0, 16, allow_small_or_imprecise_dtypes=True))
+    g.wait_ge(m.d_own, 16)
+    g_m3 = gq(g.partition_broadcast(T.tb3[:], T.tv3[0:1, :], 128))
+    g.wait_ge(m.d_tab, 32)
+    g.remote_dma_fused([RemoteDMATransfer(dst_ids=[dst_id(T.cores[q]) for q in out], dma_engine_mask=bits(off[:1]),
+                                          remote_sem=m.m_list, srcs=[T.tabd[:]], dsts=[T.tabl[place(q)] for q in out])],
+                       local_sem=m.sent)
+    rid, pid, _ = topo.addr(relay)
+    g.remote_dma(T.rtab[:], T.tabd[:], m.rl, m.sent, pid, rid, bits(on))
+    cnt["sent"] += 1 + len(on)
+
+    v(V.memset(T.inv[:], 0.0))
+    V.wait_ge(m.gq, g_b)
+    n = v(V.tensor_scalar(T.ibr[:], T.ibp[:], 15, None, AND))
+    V.wait_ge(m.v, n)
+    v(V.tensor_tensor(T.base[:], T.ibr[:], T.ibc[:], ADD))
+    V.wait_ge(m.gq, g_m3)
+    n = v(V.tensor_scalar(T.mi3[:], T.tb3[:], 0, 128, MAX, MUL))
+    V.wait_ge(m.v, n)
+    v_ix = v(V.tensor_tensor(T.ix3[:], T.mi3[:], T.ibp[:, 0:2], ADD))
+    V.wait_ge(m.d_tk2, 128)
+    v(V.tensor_scalar(T.ka[:], T.tk2[:], 15, None, AND))
+    v(V.tensor_scalar(T.kb[:], T.tk2[:], 4, None, AluOpType.arith_shift_right))
+    n = v(V.tensor_scalar(T.km[:], T.tk2[:], 0, None, AluOpType.is_lt))
+    V.wait_ge(m.v, n)
+    v(V.tensor_scalar(T.ka2[:], T.ka[:], 64, None, MUL))
+    n = v(V.tensor_tensor(T.kmu[:], T.km[:], T.ut[:], MUL))
+    V.wait_ge(m.v, n)
+    n = v(V.tensor_tensor(T.kc[:], T.ka2[:], T.kb[:], ADD))
+    V.wait_ge(m.v, n)
+    n = v(V.tensor_tensor(T.kd[:], T.kc[:], T.kmu[:], ADD))
+    V.wait_ge(m.v, n)
+    n = v(V.tensor_copy(T.so[:], T.kd[:]))
+    V.wait_ge(m.d_tok, 128)
+    v_xo = v(V.tensor_scalar(T.xo[:], T.tokb[:], 0, 4, MAX, MUL))
+    V.wait_ge(m.v, n)
+    v_inv = v(V.tensor_copy(T.inv[:, 0:1392].indirect(T.so[:, 0:16]), T.vals[:]))
+
+    def own_rows(k):
+        g.indirect_dma_start(T.go[:, 512 * k:512 * k + 512], None, T.wa[:], IndirectOffsetOnAxis(ap=T.ix3[:, k:k + 1], axis=0),
+                             bounds_check=1023).then_inc(m.d_go, 16)
+
+    g.wait_ge(m.v, v_ix)
+    own_rows(0)
+
+    pairs = [h // 2, 1 - h // 2]
+
+    def xgather(eng, pr, t):
+        a = 64 * pairs[pr]
+        win = T.xsb[:, t:4096].indirect(T.xo[:, a:a + 64])
+        dst = T.hx[:, 64 * a + t:64 * a + 4096:4]
+        if eng == "v":
+            return v(V.tensor_copy(dst, win))
+        return s(S.activation(dst, win, COPY))
+
+    def xquant(pr):
+        for a in (1024 * pairs[pr], 1024 * pairs[pr] + 512):
+            v_xq[pairs[pr]] = v(V.quantize_mx(T.xq[:, a:a + 512], T.xp[:, a:a + 512], T.hx[:, 4 * a:4 * a + 2048]))
+
+    v_xq = {}
+    S.wait_ge(m.v, v_xo)
+    S.wait_ge(m.d_x, 16)
+    xgather("s", 0, 0)
+    s_x0 = xgather("s", 0, 1)
+    xgather("s", 1, 0)
+    V.wait_ge(m.v, v_xo)
+    V.wait_ge(m.d_x, 16)
+    xgather("v", 0, 2)
+    n = xgather("v", 0, 3)
+    V.wait_ge(m.v, n)
+    V.wait_ge(m.s, s_x0)
+    xquant(0)
+
+    Y.wait_ge(m.d_x, 16)
+    for k in range(8):
+        Y.dma_start(T.wab[:, 512 * k:512 * k + 512], T.wa[128 * k:128 * k + 128, :]).then_inc(m.d_wa, 16)
+    Y.wait_ge(m.m_list, len(out))
+    Y.dma_start(T.tv1[0:1, :], T.tabl[0:6, 2 * rank:2 * rank + 2, :]).then_inc(m.d_r1, 16)
+    Y.wait_ge(m.m_nl, len(off))
+    Y.dma_start(T.tv2[0:1, :], T.tabl[6, 2 * rank:2 * rank + 2, :]).then_inc(m.d_r2, 16)
+    Y.wait_ge(m.v, v_inv)
+    for k in range(8):
+        Y.dma_start(T.e2[:, k, :], T.inv[16 * k:16 * k + 1, 0:1024]).then_inc(m.d_e1, 16)
+    Y.wait_ge(m.d_e1, 128)
+    for k in range(8):
+        Y.dma_start(T.mg[16 * k:16 * k + 16, :], T.e2[:]).then_inc(m.d_e2, 16)
+
+    g.wait_ge(m.d_r1, 16)
+    g_m1 = gq(g.partition_broadcast(T.tb1[:], T.tv1[0:1, :], 128))
+    own_rows(1)
+
+    def offsets(mf, a, dst):
+        return v(V.tensor_scalar(T.offu[:, 32 * dst:32 * dst + 32], T.base[:], mf[:, a:a + 1], None, ADD))
+
+    def agather(eng, a, b):
+        win = T.wab[:, 0:4096].indirect(T.offu[:, a // 16:b // 16])
+        if eng == "v":
+            return v(V.tensor_copy(T.ga[:, a:b], win))
+        return s(S.activation(T.ga[:, a:b], win, COPY))
+
+    V.wait_ge(m.gq, g_m1)
+    n = v(V.tensor_scalar(T.mf1[:], T.tb1[:], 0, 512, MAX, MUL))
+    V.wait_ge(m.v, n)
+    v_off = {}
+    rounds = [(0, 256), (256, 768), (768, 1280), (1280, 1792)]
+
+    def round_offsets(t):
+        if t == 3:
+            V.wait_ge(m.gq, g_m2[0])
+            w = v(V.tensor_scalar(T.mf2[:], T.tb2[:], 0, 512, MAX, MUL))
+            offsets(T.mf1, 10, 12)
+            offsets(T.mf1, 11, 13)
+            V.wait_ge(m.v, w)
+            offsets(T.mf2, 0, 10)
+            v_off[t] = offsets(T.mf2, 1, 11)
+            return
+        for k in range(rounds[t][0] // 128, rounds[t][1] // 128):
+            v_off[t] = offsets(T.mf1, k, k)
+
+    g_m2 = []
+    round_offsets(0)
+    S.wait_ge(m.d_wa, 128)
+    r0, r1 = 256 * rank, 256 * rank + 256
+    arr = m["arr%d" % rank]
+    rly = dst_id(relay)
+    for t, (c0, c2) in enumerate(rounds):
+        if t + 1 < 4:
+            round_offsets(t + 1)
+        e0, e2 = 4 * c0, 4 * c2
+        e1 = e0 + (e2 - e0) // 8 * 5
+        S.wait_ge(m.v, v_off[t])
+        s_g = agather("s", e0, e1)
+        V.wait_ge(m.v, v_off[t])
+        if t == 0:
+            V.wait_ge(m.d_wa, 128)
+        v_g = agather("v", e1, e2)
+        V.wait_ge(m.v, v_g)
+        V.wait_ge(m.s, s_g)
+        v_q = v(V.quantize_mx(T.aq[:, c0:c2], T.apl[:, c0:c2], T.ga[:, e0:e2]))
+        g.wait_ge(m.v, v_q)
+        if t == 0:
+            rid, pid, _ = topo.addr(relay)
+            g.remote_dma(T.rlc[:, 0:256].bitcast(U8), T.aq[:, c0:c2].bitcast(U8), m.rc0, m.sent, pid, rid, bits(on))
+            g.remote_dma(T.rlp[:, 0:256], T.apl[:, c0:c2], m.rs0, m.sent, pid, rid, bits(on))
+            cnt["sent"] += 2 * len(on)
+            g.wait_ge(m.d_r2, 16)
+            g_m2.append(gq(g.partition_broadcast(T.tb2[:], T.tv2[0:1, :], 128)))
+            continue
+        c1 = c0 + 256
+        to = [(dst_id(T.cores[direct[t - 1]]), off, arr, T.lc[:, r0:r1], arr, T.lp[:, r0:r1], c1, c2)]
+        if t < 3:
+            to.insert(0, (rly, inner, m["rc%d" % t], T.rlc[:, 256 * t:256 * t + 256],
+                          m["rs%d" % t], T.rlp[:, 256 * t:256 * t + 256], c0, c1))
+        else:
+            to.append((dst_id(T.cores[nbr]), inner, arr, T.lc[:, r0:r1], arr, T.lp[:, r0:r1], c0, c1))
+        g.remote_dma_fused([RemoteDMATransfer(dst_ids=[d], dma_engine_mask=bits(e), remote_sem=sc,
+                                              src=T.aq[:, a:b].bitcast(U8), dst=lc.bitcast(U8))
+                            for d, e, sc, lc, ss, lp, a, b in to], local_sem=m.sent)
+        g.remote_dma_fused([RemoteDMATransfer(dst_ids=[d], dma_engine_mask=bits(e), remote_sem=ss, src=T.apl[:, a:b], dst=lp)
+                            for d, e, sc, lc, ss, lp, a, b in to], local_sem=m.sent)
+        cnt["sent"] += 2 * (len(off) + len(inner))
+    V.wait_ge(m.d_go, 32)
+    v_o = v(V.quantize_mx(T.lc[:, r0:r1], T.lp[:, r0:r1], T.go[:]))
+
+    xgather("s", 1, 1)
+    s_x1 = xgather("s", 1, 2)
+    n = xgather("v", 1, 3)
+    V.wait_ge(m.d_e2, 128)
+    k = v(V.tensor_tensor(T.s1[:], T.mg[:, 0:256], T.mg[:, 256:512], ADD))
+    V.wait_ge(m.v, k)
+    k = v(V.tensor_tensor(T.s2[:], T.s1[:, 0:128], T.s1[:, 128:256], ADD))
+    V.wait_ge(m.v, k)
+    k = v(V.tensor_tensor(T.s3[:], T.s2[:, 0:64], T.s2[:, 64:128], ADD))
+    V.wait_ge(m.v, k)
+    v_yo = v(V.tensor_copy(T.yo[:], T.s3[:]))
+    V.wait_ge(m.s, s_x1)
+    V.wait_ge(m.v, n)
+    xquant(1)
+
+    f = [k for k in (0, 1) if dsrc[k] // 4 == rank // 4][0]
+    order = [rank, dsrc[f], rsrc[f], nbr, dsrc[1 - f], rsrc[1 - f], dsrc[2], rsrc[2]]
+    k = 0
+    freed, last = {}, {}
+    for q in order:
+        if q == rank:
+            P.wait_ge(m.v, v_o)
+        else:
+            P.wait_ge(m["arr%d" % q], 2 * len(inner if q == nbr else off))
+        P.wait_ge(m.v, v_xq[q // 4])
+        for sl in (2 * q, 2 * q + 1):
+            bank = k % 8
+            if bank in freed:
+                P.wait_ge(m[freed[bank][0]], freed[bank][1])
+            a, b = 128 * sl, 128 * sl + 128
+            prod = T.ps[:, 512 * bank:512 * bank + 128]
+            did(P.matmul_mx(prod, T.lc[:, a:b], T.lp[:, a:b], T.xq[:, a:b], T.xp[:, a:b], True, True), "p")
+            if k % 2 == 0:
+                V.wait_ge(m.p, k + 1)
+                freed[bank] = ("v", v(V.tensor_copy(T.rsb[:, a:b], prod)))
+            else:
+                S.wait_ge(m.p, k + 1)
+                freed[bank] = ("s", s(S.activation(T.rsb[:, a:b], prod, COPY)))
+            last[freed[bank][0]] = freed[bank][1]
+            k += 1
+
+    for eng in (V, S):
+        eng.wait_ge(m.v, max(v_yo, last["v"]))
+        eng.wait_ge(m.s, last["s"])
+
+    def picked(k):
+        return T.ysb[:, 256 * k:256 * k + 256], T.rsb[:, 0:2048].indirect(T.yo[:, 16 * k:16 * k + 16])
+
+    vn, sn = [], []
+    for k in range(2):
+        vn.append(v(V.tensor_copy(*picked(k))))
+        o, w = picked(2 + k)
+        sn.append(s(S.activation(o, w, COPY)))
+    for k in range(2):
+        Y.wait_ge(m.v, vn[k])
+        Y.dma_start(T.y[:, 256 * k:256 * k + 256], T.ysb[:, 256 * k:256 * k + 256]).then_inc(m.d_y, 16)
+    for k in range(2):
+        S.wait_ge(m.s, sn[k])
+        S.dma_start(T.y[:, 512 + 256 * k:768 + 256 * k], T.ysb[:, 512 + 256 * k:768 + 256 * k]).then_inc(m.d_y, 16)
+
+    g.wait_ge(m.sent, cnt["sent"])
+    g.wait_ge(m.d_y, 64)
+    g.wait_ge(m.d_go, 32)
+    for name in ("v", "s", "p", "gq"):
+        g.wait_ge(m[name], cnt[name])

@@ -2,35 +2,43 @@ from concourse.bass import DstId, RemoteDMATransfer, IndirectOffsetOnAxis
 from concourse.mybir import dt, AluOpType, ActivationFunctionType
 
 U8 = dt.uint8
-ADD, MUL, MAX, AND = AluOpType.add, AluOpType.mult, AluOpType.max, AluOpType.bitwise_and
+ADD, MUL, MAX, MIN, AND = AluOpType.add, AluOpType.mult, AluOpType.max, AluOpType.min, AluOpType.bitwise_and
 COPY = ActivationFunctionType.Copy
 
+ROUNDS = [["P0r"], ["O0r", "P1d"], ["N0r", "O1d"], ["N1d", "B0d"]]
+NAMES = [w for rnd in ROUNDS for w in rnd]
+SHARE = (9, 9, 9, 11)
+ORDER_G = "tab l0 chip l1 l2 own0 nb0 p0 c0 nb1 c1 p1 c2 p2 c3 p3 own1".split()
+ORDER_S = "x01 x02 x101 a0 a1 a2 a3 x11 x130 x100 x120 c0 c1 c3 c5 c7 c9 y2 y3".split()
+ORDER_V = ("Mb tok Mi Xo Tk Iu Ka Kb La Ix Lb Kc So x03 Inv x00 Jn o0 a0 o1 qa0 a1 o2 qa1 a2 o3 qa2 x121 a3 qa3 qn "
+           "qo0 ad0 qx1 ad1 qx0 x131 ad2 qx3 qx2 c2 ad3 qo1 c4 c6 c8 c10 y0 y1").split()
+PAIRS = 5
+Y_AT = (0, 192, 544, 800, 1024)
+
 F8 = "float8_e4m3fn_x4"
-I16 = ("sbuf", [128, 16], "int32")
-I2 = ("sbuf", [128, 2], "int32")
+I4, I16, I32 = (("sbuf", [128, n], "int32") for n in (4, 16, 32))
 SCRATCH = {
-    "tabd": ("dram", [128, 1], "int32"), "tabl": ("dram", [7, 128, 1], "int32"), "rtab": ("dram", [128, 1], "int32"),
-    "tv1": ("sbuf", [128, 12], "int32"), "tb1": ("sbuf", [128, 12], "int32"), "mf1": ("sbuf", [128, 12], "float32"),
-    "tv2": I2, "tb2": I2, "mf2": ("sbuf", [128, 2], "float32"), "tv3": I2, "tb3": I2, "mi3": I2, "ix3": I2,
-    "ibp": ("sbuf", [128, 32], "int32"), "ibc": ("sbuf", [128, 32], "int32"), "ibr": ("sbuf", [128, 32], "int32"),
-    "base": ("sbuf", [128, 32], "float32"), "offu": ("sbuf", [128, 448], "uint16"),
+    "tv": I16, "tb": I16, "mi": I4, "ix": I4, "ixn": I4, "pf": ("sbuf", [128, 2], "float32"),
+    "mb": ("sbuf", [128, 16], "bfloat16"), "ml": ("sbuf", [128, 16], "bfloat16"), "rb": ("sbuf", [128, 2], "bfloat16"),
+    "ixu": ("sbuf", [128, 4], "uint16"), "nu": ("sbuf", [128, 2], "uint16"), "pid": ("sbuf", [128, 2], "uint16"),
+    "ibp": I32, "ibc": I32, "ibr": I32, "base": ("sbuf", [128, 32], "float32"), "offu": ("sbuf", [128, 384], "uint16"),
     "tokb": ("sbuf", [128, 128], "int32"), "xo": ("sbuf", [128, 128], "uint16"),
-    "tk2": I16, "ka": I16, "kb": I16, "km": I16, "ka2": I16, "kmu": I16, "kc": I16, "kd": I16, "ut": I16,
+    "tk2": I16, "ka": I16, "kb": I16, "ka2": I16, "kb2": I16, "kc": I16, "ut": I16,
     "so": ("sbuf", [128, 16], "uint16"), "vals": ("sbuf", [128, 256], "float32"), "inv": ("sbuf", [128, 1392], "float32"),
     "e2": ("dram", [16, 8, 64], "float32"), "mg": ("sbuf", [128, 512], "float32"), "s1": ("sbuf", [128, 256], "float32"),
     "s2": ("sbuf", [128, 128], "float32"), "s3": ("sbuf", [128, 64], "float32"), "yo": ("sbuf", [128, 64], "uint16"),
     "wab": ("sbuf", [128, 4096], "bfloat16"), "xsb": ("sbuf", [128, 4096], "bfloat16"), "hx": ("sbuf", [128, 8192], "bfloat16"),
     "xq": ("sbuf", [128, 2048], F8), "xp": ("sbuf", [128, 2048], "uint8"),
-    "ga": ("sbuf", [128, 7168], "bfloat16"), "go": ("sbuf", [128, 1024], "bfloat16"),
+    "ga": ("sbuf", [128, 6144], "bfloat16"), "go": ("sbuf", [128, 1024], "bfloat16"), "gn": ("sbuf", [128, 1024], "bfloat16"),
     "aq": ("sbuf", [128, 1792], F8), "apl": ("sbuf", [128, 1792], "uint8"),
     "lc": ("sbuf", [128, 2048], F8), "lp": ("sbuf", [128, 2048], "uint8"),
     "rlc": ("sbuf", [128, 768], F8), "rlp": ("sbuf", [128, 768], "uint8"),
     "rsb": ("sbuf", [128, 2048], "float32"), "ysb": ("sbuf", [128, 1024], "float32"),
     "ps": ("psum", [128, 4096], "float32"),
 }
-SEMAPHORES = (["d_tab", "d_own", "d_x", "d_tok", "d_tk2", "d_wa", "d_e1", "d_e2", "d_r1", "d_r2", "d_y", "d_go",
-               "v", "s", "p", "gq", "sent", "m_list", "m_nl", "rl"]
-              + ["rc%d" % k for k in range(3)] + ["rs%d" % k for k in range(3)] + ["arr%d" % q for q in range(8)])
+SEMAPHORES = (["d_tab", "d_x", "d_tok", "d_wa", "d_e1", "d_e2", "d_y", "d_go0", "d_go1", "d_gn",
+               "v", "s", "p", "gq", "sent", "m_nl", "rl"] + ["ml%d" % k for k in range(4)]
+              + ["rc%d" % k for k in range(3)] + ["rp%d" % k for k in range(3)] + ["arr%d" % q for q in range(8)])
 
 
 def bits(engines):
@@ -43,333 +51,309 @@ def layout(T, topo):
         if topo.chip(c) not in chips:
             chips.append(topo.chip(c))
     ranks = [[r for r, c in enumerate(T.cores) if topo.chip(c) == ch] for ch in chips]
-    steps = sorted(range(1, len(chips)), key=lambda o: topo.same_plane(chips[0], chips[o]))
-    return chips, ranks, steps
+    lay = {}
+    for h, rs in enumerate(ranks):
+        near = [k for k in range(len(chips)) if topo.same_plane(chips[h], chips[k])][0]
+        far = [k for k in range(len(chips)) if k not in (h, near)]
+        partner = [k for k in far if k // 2 == h // 2][0]
+        other = [k for k in far if k != partner][0]
+        for i, r in enumerate(rs):
+            lay[r] = (i, {"B": rs, "P": ranks[partner], "N": ranks[near], "O": ranks[other]})
+    return lay
 
 
-def relay_of(T, topo, core, place):
-    c = [k for k in topo.cores_of(core) if topo.die(k) != topo.die(core) and T.rank_of(k) is None
-         and all(topo.may_write(k, d) for d in T.cores)]
-    return c[place]
+def peer(lay, r, w):
+    i, chips = lay[r]
+    return chips[w[0]][i if w[1] == "1" else 1 - i]
 
 
-def served(ranks, steps, h, i):
-    n = len(ranks)
-    return [ranks[(h + o) % n][1 - i] for o in steps], [ranks[(h + o) % n][i] for o in steps]
+def relay_of(T, topo, lay, r):
+    core = T.cores[r]
+    return [k for k in topo.cores_of(core) if topo.die(k) != topo.die(core) and all(topo.may_write(k, d) for d in T.cores)][lay[r][0]]
 
 
-def in_order(rl, dr):
-    return [rl[0], rl[1], dr[0], rl[2], dr[1], dr[2]]
+def engine_sets(T, topo, lay, r):
+    on = topo.engines(T.cores[r], T.cores[peer(lay, r, "B0")])
+    off = topo.engines(T.cores[r], T.cores[peer(lay, r, "P0")])
+    return on, off, [e for e in on if e not in off]
+
+
+def engines_for(sets, rnd, w):
+    on, off, inner = sets
+    if w[2] == "d" and w[0] != "B":
+        return off
+    return on if len(rnd) == 1 else inner
 
 
 def relay_program(g, core, T, topo):
-    chips, ranks, steps = layout(T, topo)
-    if topo.chip(core) not in chips:
-        return
-    h = chips.index(topo.chip(core))
-    for i, r in enumerate(ranks[h]):
-        if relay_of(T, topo, T.cores[r], i) != core:
+    lay = layout(T, topo)
+    m = T.sem
+    for r in lay:
+        if relay_of(T, topo, lay, r) != core:
             continue
-        me = T.sem
-        nb = T.cores[ranks[h][1 - i]]
-        dests = [T.cores[q] for q in served(ranks, steps, h, i)[0]]
-        eng = topo.engines(core, dests[0])
-        on = topo.engines(T.cores[r], core)
-        inner = [e for e in on if e not in topo.engines(T.cores[r], dests[0])]
-        a, b = 256 * r, 256 * r + 256
-        arr = me["arr%d" % r]
-        g.wait_ge(me.rl, len(on))
-        rid, pid, _ = topo.addr(nb)
-        g.remote_dma(T.tabl[6], T.rtab[:], me.m_nl, me.sent, pid, rid, bits(eng))
-        for k, d in enumerate(dests):
-            rid, pid, _ = topo.addr(d)
-            ins = len(inner if k else on)
-            g.wait_ge(me["rc%d" % k], ins)
-            g.remote_dma(T.lc[:, a:b].bitcast(U8), T.rlc[:, 256 * k:256 * k + 256].bitcast(U8), arr, me.sent, pid, rid, bits(eng))
-            g.wait_ge(me["rs%d" % k], ins)
-            g.remote_dma(T.lp[:, a:b], T.rlp[:, 256 * k:256 * k + 256], arr, me.sent, pid, rid, bits(eng))
-        g.wait_ge(me.sent, 7 * len(eng))
+        sets = engine_sets(T, topo, lay, r)
+        a, b, arr = 256 * r, 256 * r + 256, m["arr%d" % r]
+        to = T.cores[peer(lay, r, NAMES[5])]
+        rid, pid, _ = topo.addr(to)
+        eng = topo.engines(core, to)
+        g.wait_ge(m.rl, len(sets[2]) // 2)
+        g.remote_dma(T.ml[:, 10:12], T.rb[:], m.ml3, m.sent, pid, rid, bits(eng))
+        for t in [t for t in ORDER_G if t[0] in "cp" and t[1:].isdigit()]:
+            k = int(t[1])
+            w = ROUNDS[k][0]
+            if w[2] != "r":
+                continue
+            rid, pid, _ = topo.addr(T.cores[peer(lay, r, w)])
+            g.wait_ge(m["r" + t], len(engines_for(sets, ROUNDS[k], w)))
+            if t[0] == "c":
+                g.remote_dma(T.lc[:, a:b].bitcast(U8), T.rlc[:, 256 * k:256 * k + 256].bitcast(U8), arr, m.sent, pid, rid, bits(eng))
+            else:
+                g.remote_dma(T.lp[:, a:b], T.rlp[:, 256 * k:256 * k + 256], arr, m.sent, pid, rid, bits(eng))
+        g.wait_ge(m.sent, 7 * len(eng))
 
 
 def rank_program(g, core, T, topo):
     rank = T.rank_of(core)
     if rank is None:
         return relay_program(g, core, T, topo)
-    chips, ranks, steps = layout(T, topo)
-    C = len(chips)
-    h = chips.index(topo.chip(core))
-    i = ranks[h].index(rank)
-    nbr = ranks[h][1 - i]
-    relay = relay_of(T, topo, core, i)
-    relayed, direct = served(ranks, steps, h, i)
-    out = in_order(relayed, direct)
-    rsrc = [ranks[(h - o) % C][1 - i] for o in steps]
-    dsrc = [ranks[(h - o) % C][i] for o in steps]
-    on = topo.engines(core, relay)
-    off = topo.engines(core, T.cores[out[0]])
-    inner = [e for e in on if e not in off]
+    lay = layout(T, topo)
+    i, chips = lay[rank]
+    out = [peer(lay, rank, w) for w in NAMES]
+    nbr, relay = out[6], relay_of(T, topo, lay, rank)
+    sets = engine_sets(T, topo, lay, rank)
+    on, off, inner = sets
     S, V, P, Y = g.scalar, g.vector, g.tensor, g.sync
     m = T.sem
     cnt = {"v": 0, "s": 0, "p": 0, "gq": 0, "sent": 0}
+    seen = {}
 
     def did(ins, name):
         ins.then_inc(m[name], 1)
         cnt[name] += 1
         return cnt[name]
 
+    def wait(queue, name, n):
+        if seen.get((queue, name), 0) < n:
+            seen[queue, name] = n
+            {"v": V, "s": S, "p": P, "g": g, "y": Y}[queue].wait_ge(m[name], n)
+
     def v(ins): return did(ins, "v")
-    def s(ins): return did(ins, "s")
     def gq(ins): return did(ins, "gq")
 
     def dst_id(c):
         rid, pid, _ = topo.addr(c)
         return DstId(rid=rid, pnc=pid)
 
-    def place(q):
-        hq = [k for k in range(C) if q in ranks[k]][0]
-        return in_order(*served(ranks, steps, hq, ranks[hq].index(q))).index(rank)
+    def write(c, engines, sem, src, dst):
+        cnt["sent"] += len(engines)
+        return RemoteDMATransfer(dst_ids=[dst_id(c)], dma_engine_mask=bits(engines), remote_sem=m[sem], src=src, dst=dst)
 
-    def tok_loads(eng, ks):
-        for k in ks:
-            eng.dma_start(T.tk2[16 * k:16 * k + 16, :], T.tok[:, 16 * k:16 * k + 16]).then_inc(m.d_tk2, 16)
-        for k in ks:
-            eng.dma_start(T.tokb[16 * k:16 * k + 16, :], T.tok[:]).then_inc(m.d_tok, 16)
-
-    Y.dma_start(T.tabd[0:16, :], T.tab[:]).then_inc(m.d_tab, 16)
-    Y.dma_start(T.tabd[16:128, :], T.tok[0:1, 0:112]).then_inc(m.d_tab, 16)
-    S.dma_start(T.tv3[0:1, :], T.tab[2 * rank:2 * rank + 2, :]).then_inc(m.d_own, 16)
-    tok_loads(Y, range(0, 4))
-    tok_loads(S, range(4, 8))
+    lo = min(rank, nbr)
+    Y.dma_start(T.tv[0:1, :], T.tab[:]).then_inc(m.d_tab, 16)
+    for k in range(4):
+        (Y if k < 2 else S).dma_start(T.tokb[16 * k:16 * k + 16, :], T.tok[:]).then_inc(m.d_tok, 16)
     Y.dma_start(T.xsb[:], T.x[:]).then_inc(m.d_x, 16)
-    gq(g.iota(T.ut[:], [[16, 16]], 65, 1))
-    gq(g.iota(T.ibp[:], [[0, 32]], 0, 1))
-    gq(g.iota(T.ibc[:], [[16, 32]], 0, 0))
-    g_b = gq(g.iota(T.vals[:], [[1, 256]], 0, 16, allow_small_or_imprecise_dtypes=True))
-    g.wait_ge(m.d_own, 16)
-    g_m3 = gq(g.partition_broadcast(T.tb3[:], T.tv3[0:1, :], 128))
-    g.wait_ge(m.d_tab, 32)
-    g.remote_dma_fused([RemoteDMATransfer(dst_ids=[dst_id(T.cores[q]) for q in out], dma_engine_mask=bits(off[:1]),
-                                          remote_sem=m.m_list, srcs=[T.tabd[:]], dsts=[T.tabl[place(q)] for q in out])],
-                       local_sem=m.sent)
-    rid, pid, _ = topo.addr(relay)
-    g.remote_dma(T.rtab[:], T.tabd[:], m.rl, m.sent, pid, rid, bits(on))
-    cnt["sent"] += 1 + len(on)
-
-    v(V.memset(T.inv[:], 0.0))
-    V.wait_ge(m.gq, g_b)
-    n = v(V.tensor_scalar(T.ibr[:], T.ibp[:], 15, None, AND))
-    V.wait_ge(m.v, n)
-    v(V.tensor_tensor(T.base[:], T.ibr[:], T.ibc[:], ADD))
-    V.wait_ge(m.gq, g_m3)
-    n = v(V.tensor_scalar(T.mi3[:], T.tb3[:], 0, 128, MAX, MUL))
-    V.wait_ge(m.v, n)
-    v_ix = v(V.tensor_tensor(T.ix3[:], T.mi3[:], T.ibp[:, 0:2], ADD))
-    V.wait_ge(m.d_tk2, 128)
-    v(V.tensor_scalar(T.ka[:], T.tk2[:], 15, None, AND))
-    v(V.tensor_scalar(T.kb[:], T.tk2[:], 4, None, AluOpType.arith_shift_right))
-    n = v(V.tensor_scalar(T.km[:], T.tk2[:], 0, None, AluOpType.is_lt))
-    V.wait_ge(m.v, n)
-    v(V.tensor_scalar(T.ka2[:], T.ka[:], 64, None, MUL))
-    n = v(V.tensor_tensor(T.kmu[:], T.km[:], T.ut[:], MUL))
-    V.wait_ge(m.v, n)
-    n = v(V.tensor_tensor(T.kc[:], T.ka2[:], T.kb[:], ADD))
-    V.wait_ge(m.v, n)
-    n = v(V.tensor_tensor(T.kd[:], T.kc[:], T.kmu[:], ADD))
-    V.wait_ge(m.v, n)
-    n = v(V.tensor_copy(T.so[:], T.kd[:]))
-    V.wait_ge(m.d_tok, 128)
-    v_xo = v(V.tensor_scalar(T.xo[:], T.tokb[:], 0, 4, MAX, MUL))
-    V.wait_ge(m.v, n)
-    v_inv = v(V.tensor_copy(T.inv[:, 0:1392].indirect(T.so[:, 0:16]), T.vals[:]))
-
-    def own_rows(k):
-        g.indirect_dma_start(T.go[:, 512 * k:512 * k + 512], None, T.wa[:], IndirectOffsetOnAxis(ap=T.ix3[:, k:k + 1], axis=0),
-                             bounds_check=1023).then_inc(m.d_go, 16)
-
-    g.wait_ge(m.v, v_ix)
-    own_rows(0)
-
-    pairs = [h // 2, 1 - h // 2]
-
-    def xgather(eng, pr, t):
-        a = 64 * pairs[pr]
-        win = T.xsb[:, t:4096].indirect(T.xo[:, a:a + 64])
-        dst = T.hx[:, 64 * a + t:64 * a + 4096:4]
-        if eng == "v":
-            return v(V.tensor_copy(dst, win))
-        return s(S.activation(dst, win, COPY))
-
-    def xquant(pr):
-        for a in (1024 * pairs[pr], 1024 * pairs[pr] + 512):
-            v_xq[pairs[pr]] = v(V.quantize_mx(T.xq[:, a:a + 512], T.xp[:, a:a + 512], T.hx[:, 4 * a:4 * a + 2048]))
-
-    v_xq = {}
-    S.wait_ge(m.v, v_xo)
-    S.wait_ge(m.d_x, 16)
-    xgather("s", 0, 0)
-    s_x0 = xgather("s", 0, 1)
-    xgather("s", 1, 0)
-    V.wait_ge(m.v, v_xo)
-    V.wait_ge(m.d_x, 16)
-    xgather("v", 0, 2)
-    n = xgather("v", 0, 3)
-    V.wait_ge(m.v, n)
-    V.wait_ge(m.s, s_x0)
-    xquant(0)
-
-    Y.wait_ge(m.d_x, 16)
     for k in range(8):
         Y.dma_start(T.wab[:, 512 * k:512 * k + 512], T.wa[128 * k:128 * k + 128, :]).then_inc(m.d_wa, 16)
-    Y.wait_ge(m.m_list, len(out))
-    Y.dma_start(T.tv1[0:1, :], T.tabl[0:6, 2 * rank:2 * rank + 2, :]).then_inc(m.d_r1, 16)
-    Y.wait_ge(m.m_nl, len(off))
-    Y.dma_start(T.tv2[0:1, :], T.tabl[6, 2 * rank:2 * rank + 2, :]).then_inc(m.d_r2, 16)
-    Y.wait_ge(m.v, v_inv)
+
+    gq(g.iota(T.ibp[:], [[0, 32]], 0, 1))
+    g_a = gq(g.iota(T.ibc[:], [[16, 32]], 0, 0))
+    gq(g.iota(T.ut[:], [[16, 16]], 64, 1))
+    g_b = gq(g.iota(T.vals[:], [[1, 256]], 0, 16, allow_small_or_imprecise_dtypes=True))
+    v(V.memset(T.inv[:, 0:1024], 0.0))
+    wait("v", "gq", g_a)
+    n = v(V.tensor_scalar(T.ibr[:], T.ibp[:], 15, None, AND))
+    v(V.tensor_copy(T.pid[:], T.ibp[:, 0:2]))
+    v(V.tensor_copy(T.pf[:], T.ibp[:, 0:2]))
+    wait("v", "v", n)
+    v_pre = v(V.tensor_tensor(T.base[:], T.ibr[:], T.ibc[:], ADD))
+
+    outer = {"tab": ("gq", g_b + 1), "iota": ("gq", g_b), "d_tok": ("d_tok", 64), "e2": ("d_e2", 128), "nl": ("m_nl", len(inner) // 2)}
+    small = {
+        "Mb": (["tab"], lambda: V.tensor_scalar(T.mb[:], T.tb[:], 0, 512, MAX, MUL)),
+        "Mi": (["tab"], lambda: V.tensor_scalar(T.mi[:], T.tb[:, 2 * lo:2 * lo + 4], 0, 128, MAX, MUL)),
+        "Iu": (["Mi"], lambda: V.tensor_scalar(T.ixu[:], T.mi[:], T.pf[:, 0:1], None, ADD)),
+        "Ix": (["Mi"], lambda: V.tensor_scalar(T.ix[:], T.mi[:], T.pf[:, 0:1], None, ADD)),
+        "Jn": (["nl"], lambda: V.tensor_copy(T.ixn[:, 0:2], T.nu[:])),
+        "tok": (["d_tok"], lambda: V.tensor_copy(T.tokb[64:128, :], T.tokb[0:64, :])),
+        "Xo": (["tok"], lambda: V.tensor_scalar(T.xo[:], T.tokb[:], 0, 4, MAX, MUL)),
+        "Tk": (["tok"], lambda: V.tensor_copy(T.tk2[:], T.tokb[:, 0:128].indirect(T.pid[:, 0:1]))),
+        "Ka": (["Tk"], lambda: V.tensor_scalar(T.ka[:], T.tk2[:], 15, None, AND)),
+        "Kb": (["Tk"], lambda: V.tensor_scalar(T.kb[:], T.tk2[:], 4, None, AluOpType.logical_shift_right)),
+        "La": (["Ka"], lambda: V.tensor_scalar(T.ka2[:], T.ka[:], 64, None, MUL)),
+        "Lb": (["Kb", "iota"], lambda: V.tensor_tensor(T.kb2[:], T.kb[:], T.ut[:], MIN)),
+        "Kc": (["La", "Lb"], lambda: V.tensor_tensor(T.kc[:], T.ka2[:], T.kb2[:], ADD)),
+        "So": (["Kc"], lambda: V.tensor_copy(T.so[:], T.kc[:])),
+        "Inv": (["So"], lambda: V.tensor_copy(T.inv[:, 0:1392].indirect(T.so[:, 0:16]), T.vals[:])),
+        "ad0": (["e2"], lambda: V.tensor_tensor(T.s1[:], T.mg[:, 0:256], T.mg[:, 256:512], ADD)),
+        "ad1": (["ad0"], lambda: V.tensor_tensor(T.s2[:], T.s1[:, 0:128], T.s1[:, 128:256], ADD)),
+        "ad2": (["ad1"], lambda: V.tensor_tensor(T.s3[:], T.s2[:, 0:64], T.s2[:, 64:128], ADD)),
+        "ad3": (["ad2"], lambda: V.tensor_copy(T.yo[:], T.s3[:])),
+    }
+
+    arrive = [peer(lay, rank, w) for w in ("P1", "P0", "O1", "O0", "N1", "B0", "N0")]
+    groups = [[2 * rank]] + [[2 * q, 2 * q + 1] for q in arrive[:PAIRS]]
+    groups += [[sl] for q in arrive[PAIRS:] for sl in (2 * q, 2 * q + 1)] + [[2 * rank + 1]]
+    ends = [sum(len(x) for x in groups[:k + 1]) for k in range(len(groups))]
+    halves = [rank // 4, 1 - rank // 4]
+    xchips = [chips[c] for c in "BPNO"]
+    cols = [(256 * NAMES.index(rnd[0]), 256 * NAMES.index([w for w in rnd if w[0] != "B"][-1]) + 256) for rnd in ROUNDS]
+    r0, r1 = 256 * rank, 256 * rank + 256
+
+    todo = {"v": ORDER_V, "s": ORDER_S}
+    done = {}
+    for e in "vs":
+        c = cnt[e]
+        for t in todo[e]:
+            c += (cols[int(t[1])][1] - cols[int(t[1])][0]) // 128 if t[0] == "o" else 1
+            done[e, t] = c
+
+    def need(queue, t):
+        for e in "vs":
+            if (e, t) in done:
+                wait(queue, e, done[e, t])
+
+    def move(e, dst, src):
+        did(V.tensor_copy(dst, src) if e == "v" else S.activation(dst, src, COPY), e)
+
+    def emit(e, t):
+        if t in small:
+            wait(e, "v", v_pre)
+            for d in small[t][0]:
+                if d in outer:
+                    wait(e, *outer[d])
+                need(e, d)
+            v(small[t][1]())
+        elif t[0] == "x":
+            a, el = 64 * halves[int(t[1])], int(t[2])
+            b = a + 64
+            if len(t) > 3:
+                a = 16 * xchips[2 * int(t[1]) + int(t[3])][0]
+                b = a + 32
+            need(e, "Xo")
+            wait(e, "d_x", 16)
+            move(e, T.hx[:, 64 * a + el:64 * b:4], T.xsb[:, el:4096].indirect(T.xo[:, a:b]))
+        elif t[:2] == "qx":
+            c = int(t[2])
+            for el in range(4):
+                need(e, "x%d%d" % (c // 2, el))
+                need(e, "x%d%d%d" % (c // 2, el, c % 2))
+            a = 256 * xchips[c][0]
+            v(V.quantize_mx(T.xq[:, a:a + 512], T.xp[:, a:a + 512], T.hx[:, 4 * a:4 * a + 2048]))
+        elif t[0] == "o":
+            c0, c1 = cols[int(t[1])]
+            for k in range(c0 // 128, c1 // 128):
+                wait(e, "ml%d" % (3 if k >= 10 else k // 4), len(off))
+                v(V.tensor_scalar(T.offu[:, 32 * k:32 * k + 32], T.base[:], T.ml[:, k:k + 1], None, ADD))
+        elif t[0] == "a":
+            c0, c1 = cols[int(t[1])]
+            cut = 4 * c0 + (c1 - c0) // 4 * SHARE[int(t[1])]
+            a, b = (4 * c0, cut) if e == "s" else (cut, 4 * c1)
+            need(e, "o" + t[1])
+            wait(e, "d_wa", 128)
+            move(e, T.ga[:, a:b], T.wab[:, 0:4096].indirect(T.offu[:, a // 16:b // 16]))
+        elif t[:2] == "qa":
+            c0, c1 = cols[int(t[2])]
+            need(e, t[1:])
+            v(V.quantize_mx(T.aq[:, c0:c1], T.apl[:, c0:c1], T.ga[:, 4 * c0:4 * c1]))
+        elif t == "qn":
+            wait(e, "d_gn", 32)
+            v(V.quantize_mx(T.aq[:, 1536:1792], T.apl[:, 1536:1792], T.gn[:]))
+        elif t[:2] == "qo":
+            k = int(t[2])
+            a = r0 + 128 * k
+            wait(e, "d_go%d" % k, 16)
+            v(V.quantize_mx(T.lc[:, a:a + 128], T.lp[:, a:a + 128], T.go[:, 512 * k:512 * k + 512]))
+        elif t[0] == "c":
+            k = int(t[1:])
+            a, n = 128 * groups[k][0], 128 * len(groups[k])
+            wait(e, "p", ends[k])
+            move(e, T.rsb[:, a:a + n], T.ps[:, 512 * (k % 8):512 * (k % 8) + n])
+        else:
+            a, b = Y_AT[int(t[1])], Y_AT[int(t[1]) + 1]
+            need(e, "ad3")
+            for k in range(len(groups)):
+                need(e, "c%d" % k)
+            move(e, T.ysb[:, a:b], T.rsb[:, 0:2048].indirect(T.yo[:, a // 16:b // 16]))
+
+    for e in "vs":
+        for t in todo[e]:
+            emit(e, t)
+
+    def rows(dst, ix, k, sem):
+        g.indirect_dma_start(dst[:, 512 * k:512 * k + 512], None, T.wa[:], IndirectOffsetOnAxis(ap=ix, axis=0),
+                             bounds_check=1023).then_inc(m[sem], 16)
+
+    def entries(q):
+        return T.mb[:, 2 * q:2 * q + 2]
+
+    for t in ORDER_G:
+        if t == "tab":
+            wait("g", "d_tab", 16)
+            gq(g.partition_broadcast(T.tb[:], T.tv[0:1, :], 128))
+        elif t == "chip":
+            need("g", "Iu")
+            h = len(inner) // 2
+            g.remote_dma_fused([write(T.cores[nbr], inner[:h], "m_nl", T.ixu[:, 2 - 2 * i:4 - 2 * i], T.nu[:]),
+                                write(relay, inner[h:], "rl", entries(out[5]), T.rb[:])], local_sem=m.sent)
+        elif t[0] == "l":
+            need("g", "Mb")
+            js = [j for j in (2 * int(t[1]), 2 * int(t[1]) + 1) if j < 5]
+            h = len(off) // len(js)
+            g.remote_dma_fused([write(T.cores[out[j]], off[h * (j % 2):h * (j % 2) + h], "m" + t, entries(out[j]), T.ml[:, 2 * j:2 * j + 2])
+                                for j in js], local_sem=m.sent)
+        elif t[:3] == "own":
+            k = int(t[3])
+            need("g", "Ix")
+            rows(T.go, T.ix[:, 2 * i + k:2 * i + k + 1], k, "d_go%d" % k)
+        elif t[:2] == "nb":
+            k = int(t[2])
+            need("g", "Jn")
+            rows(T.gn, T.ixn[:, k:k + 1], k, "d_gn")
+        else:
+            k = int(t[1])
+            need("g", "qa%d" % k)
+            to = []
+            for w in ROUNDS[k]:
+                if w[0] == "B":
+                    need("g", "qn")
+                a = 256 * NAMES.index(w)
+                if w[2] == "r":
+                    c, sem, codes, planes = relay, "r" + t, T.rlc[:, 256 * k:256 * k + 256], T.rlp[:, 256 * k:256 * k + 256]
+                else:
+                    c, sem, codes, planes = T.cores[peer(lay, rank, w)], "arr%d" % rank, T.lc[:, r0:r1], T.lp[:, r0:r1]
+                src, dst = (T.aq[:, a:a + 256].bitcast(U8), codes.bitcast(U8)) if t[0] == "c" else (T.apl[:, a:a + 256], planes)
+                to.append(write(c, engines_for(sets, ROUNDS[k], w), sem, src, dst))
+            g.remote_dma_fused(to, local_sem=m.sent)
+
+    need("y", "Inv")
     for k in range(8):
         Y.dma_start(T.e2[:, k, :], T.inv[16 * k:16 * k + 1, 0:1024]).then_inc(m.d_e1, 16)
-    Y.wait_ge(m.d_e1, 128)
+    wait("y", "d_e1", 128)
     for k in range(8):
         Y.dma_start(T.mg[16 * k:16 * k + 16, :], T.e2[:]).then_inc(m.d_e2, 16)
+    for queue, q, k in (("y", Y, 0), ("y", Y, 2), ("y", Y, 1), ("s", S, 3)):
+        need(queue, "y%d" % k)
+        q.dma_start(T.y[:, Y_AT[k]:Y_AT[k + 1]], T.ysb[:, Y_AT[k]:Y_AT[k + 1]]).then_inc(m.d_y, 16)
 
-    g.wait_ge(m.d_r1, 16)
-    g_m1 = gq(g.partition_broadcast(T.tb1[:], T.tv1[0:1, :], 128))
-    own_rows(1)
-
-    def offsets(mf, a, dst):
-        return v(V.tensor_scalar(T.offu[:, 32 * dst:32 * dst + 32], T.base[:], mf[:, a:a + 1], None, ADD))
-
-    def agather(eng, a, b):
-        win = T.wab[:, 0:4096].indirect(T.offu[:, a // 16:b // 16])
-        if eng == "v":
-            return v(V.tensor_copy(T.ga[:, a:b], win))
-        return s(S.activation(T.ga[:, a:b], win, COPY))
-
-    V.wait_ge(m.gq, g_m1)
-    n = v(V.tensor_scalar(T.mf1[:], T.tb1[:], 0, 512, MAX, MUL))
-    V.wait_ge(m.v, n)
-    v_off = {}
-    rounds = [(0, 256), (256, 768), (768, 1280), (1280, 1792)]
-
-    def round_offsets(t):
-        if t == 3:
-            V.wait_ge(m.gq, g_m2[0])
-            w = v(V.tensor_scalar(T.mf2[:], T.tb2[:], 0, 512, MAX, MUL))
-            offsets(T.mf1, 10, 12)
-            offsets(T.mf1, 11, 13)
-            V.wait_ge(m.v, w)
-            offsets(T.mf2, 0, 10)
-            v_off[t] = offsets(T.mf2, 1, 11)
-            return
-        for k in range(rounds[t][0] // 128, rounds[t][1] // 128):
-            v_off[t] = offsets(T.mf1, k, k)
-
-    g_m2 = []
-    round_offsets(0)
-    S.wait_ge(m.d_wa, 128)
-    r0, r1 = 256 * rank, 256 * rank + 256
-    arr = m["arr%d" % rank]
-    rly = dst_id(relay)
-    for t, (c0, c2) in enumerate(rounds):
-        if t + 1 < 4:
-            round_offsets(t + 1)
-        e0, e2 = 4 * c0, 4 * c2
-        e1 = e0 + (e2 - e0) // 8 * 5
-        S.wait_ge(m.v, v_off[t])
-        s_g = agather("s", e0, e1)
-        V.wait_ge(m.v, v_off[t])
-        if t == 0:
-            V.wait_ge(m.d_wa, 128)
-        v_g = agather("v", e1, e2)
-        V.wait_ge(m.v, v_g)
-        V.wait_ge(m.s, s_g)
-        v_q = v(V.quantize_mx(T.aq[:, c0:c2], T.apl[:, c0:c2], T.ga[:, e0:e2]))
-        g.wait_ge(m.v, v_q)
-        if t == 0:
-            rid, pid, _ = topo.addr(relay)
-            g.remote_dma(T.rlc[:, 0:256].bitcast(U8), T.aq[:, c0:c2].bitcast(U8), m.rc0, m.sent, pid, rid, bits(on))
-            g.remote_dma(T.rlp[:, 0:256], T.apl[:, c0:c2], m.rs0, m.sent, pid, rid, bits(on))
-            cnt["sent"] += 2 * len(on)
-            g.wait_ge(m.d_r2, 16)
-            g_m2.append(gq(g.partition_broadcast(T.tb2[:], T.tv2[0:1, :], 128)))
-            continue
-        c1 = c0 + 256
-        to = [(dst_id(T.cores[direct[t - 1]]), off, arr, T.lc[:, r0:r1], arr, T.lp[:, r0:r1], c1, c2)]
-        if t < 3:
-            to.insert(0, (rly, inner, m["rc%d" % t], T.rlc[:, 256 * t:256 * t + 256],
-                          m["rs%d" % t], T.rlp[:, 256 * t:256 * t + 256], c0, c1))
-        else:
-            to.append((dst_id(T.cores[nbr]), inner, arr, T.lc[:, r0:r1], arr, T.lp[:, r0:r1], c0, c1))
-        g.remote_dma_fused([RemoteDMATransfer(dst_ids=[d], dma_engine_mask=bits(e), remote_sem=sc,
-                                              src=T.aq[:, a:b].bitcast(U8), dst=lc.bitcast(U8))
-                            for d, e, sc, lc, ss, lp, a, b in to], local_sem=m.sent)
-        g.remote_dma_fused([RemoteDMATransfer(dst_ids=[d], dma_engine_mask=bits(e), remote_sem=ss, src=T.apl[:, a:b], dst=lp)
-                            for d, e, sc, lc, ss, lp, a, b in to], local_sem=m.sent)
-        cnt["sent"] += 2 * (len(off) + len(inner))
-    V.wait_ge(m.d_go, 32)
-    v_o = v(V.quantize_mx(T.lc[:, r0:r1], T.lp[:, r0:r1], T.go[:]))
-
-    xgather("s", 1, 1)
-    s_x1 = xgather("s", 1, 2)
-    n = xgather("v", 1, 3)
-    V.wait_ge(m.d_e2, 128)
-    k = v(V.tensor_tensor(T.s1[:], T.mg[:, 0:256], T.mg[:, 256:512], ADD))
-    V.wait_ge(m.v, k)
-    k = v(V.tensor_tensor(T.s2[:], T.s1[:, 0:128], T.s1[:, 128:256], ADD))
-    V.wait_ge(m.v, k)
-    k = v(V.tensor_tensor(T.s3[:], T.s2[:, 0:64], T.s2[:, 64:128], ADD))
-    V.wait_ge(m.v, k)
-    v_yo = v(V.tensor_copy(T.yo[:], T.s3[:]))
-    V.wait_ge(m.s, s_x1)
-    V.wait_ge(m.v, n)
-    xquant(1)
-
-    f = [k for k in (0, 1) if dsrc[k] // 4 == rank // 4][0]
-    order = [rank, dsrc[f], rsrc[f], nbr, dsrc[1 - f], rsrc[1 - f], dsrc[2], rsrc[2]]
-    k = 0
-    freed, last = {}, {}
-    for q in order:
+    for k, grp in enumerate(groups):
+        q = grp[0] // 2
         if q == rank:
-            P.wait_ge(m.v, v_o)
+            need("p", "qo%d" % (grp[0] % 2))
         else:
-            P.wait_ge(m["arr%d" % q], 2 * len(inner if q == nbr else off))
-        P.wait_ge(m.v, v_xq[q // 4])
-        for sl in (2 * q, 2 * q + 1):
-            bank = k % 8
-            if bank in freed:
-                P.wait_ge(m[freed[bank][0]], freed[bank][1])
-            a, b = 128 * sl, 128 * sl + 128
-            prod = T.ps[:, 512 * bank:512 * bank + 128]
-            did(P.matmul_mx(prod, T.lc[:, a:b], T.lp[:, a:b], T.xq[:, a:b], T.xp[:, a:b], True, True), "p")
-            if k % 2 == 0:
-                V.wait_ge(m.p, k + 1)
-                freed[bank] = ("v", v(V.tensor_copy(T.rsb[:, a:b], prod)))
-            else:
-                S.wait_ge(m.p, k + 1)
-                freed[bank] = ("s", s(S.activation(T.rsb[:, a:b], prod, COPY)))
-            last[freed[bank][0]] = freed[bank][1]
-            k += 1
-
-    for eng in (V, S):
-        eng.wait_ge(m.v, max(v_yo, last["v"]))
-        eng.wait_ge(m.s, last["s"])
-
-    def picked(k):
-        return T.ysb[:, 256 * k:256 * k + 256], T.rsb[:, 0:2048].indirect(T.yo[:, 16 * k:16 * k + 16])
-
-    vn, sn = [], []
-    for k in range(2):
-        vn.append(v(V.tensor_copy(*picked(k))))
-        o, w = picked(2 + k)
-        sn.append(s(S.activation(o, w, COPY)))
-    for k in range(2):
-        Y.wait_ge(m.v, vn[k])
-        Y.dma_start(T.y[:, 256 * k:256 * k + 256], T.ysb[:, 256 * k:256 * k + 256]).then_inc(m.d_y, 16)
-    for k in range(2):
-        S.wait_ge(m.s, sn[k])
-        S.dma_start(T.y[:, 512 + 256 * k:768 + 256 * k], T.ysb[:, 512 + 256 * k:768 + 256 * k]).then_inc(m.d_y, 16)
+            wait("p", "arr%d" % q, 2 * len(inner if q == nbr else off))
+        need("p", "qx%d" % [q in c for c in xchips].index(True))
+        if k >= 8:
+            need("p", "c%d" % (k - 8))
+        a = 128 * grp[0]
+        for sl in reversed(grp):
+            w, b = 128 * sl, 128 * sl + 128
+            if sl != grp[-1]:
+                wait("p", "p", cnt["p"])
+            did(P.matmul_mx(T.ps[:, 512 * (k % 8):512 * (k % 8) + b - a], T.lc[:, w:b], T.lp[:, w:b], T.xq[:, a:b], T.xp[:, a:b],
+                            True, True), "p")
 
     g.wait_ge(m.sent, cnt["sent"])
     g.wait_ge(m.d_y, 64)
-    g.wait_ge(m.d_go, 32)
     for name in ("v", "s", "p", "gq"):
         g.wait_ge(m[name], cnt[name])

from concourse.bass import DstId, RemoteDMATransfer, IndirectOffsetOnAxis
from concourse.mybir import dt, AluOpType, ActivationFunctionType

U8 = dt.uint8
ADD, MUL, MAX, MIN, AND = AluOpType.add, AluOpType.mult, AluOpType.max, AluOpType.min, AluOpType.bitwise_and
COPY = ActivationFunctionType.Copy

ROUNDS = [["P0r"], ["O0r", "P1d"], ["N0r", "O1d"], ["N1d", "B0d"]]
NAMES = [w for rnd in ROUNDS for w in rnd]
SHARE = (9, 9, 9, 11)
ORDER_G = "tab l0 chip l1 l2 own0 nb0 p0 c0 nb1 c1 p1 c2 p2 c3 p3 own1".split()
ORDER_S = "x01 x02 x101 a0 a1 a2 a3 x11 x130 x100 x120 c0 c1 c3 c5 c7 c9 y2 y3".split()
ORDER_V = ("Mb tok Mi Xo Tk Iu Ka Kb La Ix Lb Kc So x03 Inv x00 Jn o0 a0 o1 qa0 a1 o2 qa1 a2 o3 qa2 x121 a3 qa3 qn "
           "qo0 ad0 qx1 ad1 qx0 x131 ad2 qx3 qx2 c2 ad3 qo1 c4 c6 c8 c10 y0 y1").split()
PAIRS = 5
Y_AT = (0, 192, 544, 800, 1024)

F8 = "float8_e4m3fn_x4"
I4, I16, I32 = (("sbuf", [128, n], "int32") for n in (4, 16, 32))
SCRATCH = {
    "tv": I16, "tb": I16, "mi": I4, "ix": I4, "ixn": I4, "pf": ("sbuf", [128, 2], "float32"),
    "mb": ("sbuf", [128, 16], "bfloat16"), "ml": ("sbuf", [128, 16], "bfloat16"), "rb": ("sbuf", [128, 2], "bfloat16"),
    "ixu": ("sbuf", [128, 4], "uint16"), "nu": ("sbuf", [128, 2], "uint16"), "pid": ("sbuf", [128, 2], "uint16"),
    "ibp": I32, "ibc": I32, "ibr": I32, "base": ("sbuf", [128, 32], "float32"), "offu": ("sbuf", [128, 384], "uint16"),
    "tokb": ("sbuf", [128, 128], "int32"), "xo": ("sbuf", [128, 128], "uint16"),
    "tk2": I16, "ka": I16, "kb": I16, "ka2": I16, "kb2": I16, "kc": I16, "ut": I16,
    "so": ("sbuf", [128, 16], "uint16"), "vals": ("sbuf", [128, 256], "float32"), "inv": ("sbuf", [128, 1392], "float32"),
    "e2": ("dram", [16, 8, 64], "float32"), "mg": ("sbuf", [128, 512], "float32"), "s1": ("sbuf", [128, 256], "float32"),
    "s2": ("sbuf", [128, 128], "float32"), "s3": ("sbuf", [128, 64], "float32"), "yo": ("sbuf", [128, 64], "uint16"),
    "wab": ("sbuf", [128, 4096], "bfloat16"), "xsb": ("sbuf", [128, 4096], "bfloat16"), "hx": ("sbuf", [128, 8192], "bfloat16"),
    "xq": ("sbuf", [128, 2048], F8), "xp": ("sbuf", [128, 2048], "uint8"),
    "ga": ("sbuf", [128, 6144], "bfloat16"), "go": ("sbuf", [128, 1024], "bfloat16"), "gn": ("sbuf", [128, 1024], "bfloat16"),
    "aq": ("sbuf", [128, 1792], F8), "apl": ("sbuf", [128, 1792], "uint8"),
    "lc": ("sbuf", [128, 2048], F8), "lp": ("sbuf", [128, 2048], "uint8"),
    "rlc": ("sbuf", [128, 768], F8), "rlp": ("sbuf", [128, 768], "uint8"),
    "rsb": ("sbuf", [128, 2048], "float32"), "ysb": ("sbuf", [128, 1024], "float32"),
    "ps": ("psum", [128, 4096], "float32"),
}
SEMAPHORES = (["d_tab", "d_x", "d_tok", "d_wa", "d_e1", "d_e2", "d_y", "d_go0", "d_go1", "d_gn",
               "v", "s", "p", "gq", "sent", "m_nl", "rl"] + ["ml%d" % k for k in range(4)]
              + ["rc%d" % k for k in range(3)] + ["rp%d" % k for k in range(3)] + ["arr%d" % q for q in range(8)])


def bits(engines):
    return sum(1 << e for e in engines)


def layout(T, topo):
    chips = []
    for c in T.cores:
        if topo.chip(c) not in chips:
            chips.append(topo.chip(c))
    ranks = [[r for r, c in enumerate(T.cores) if topo.chip(c) == ch] for ch in chips]
    lay = {}
    for h, rs in enumerate(ranks):
        near = [k for k in range(len(chips)) if topo.same_plane(chips[h], chips[k])][0]
        far = [k for k in range(len(chips)) if k not in (h, near)]
        partner = [k for k in far if k // 2 == h // 2][0]
        other = [k for k in far if k != partner][0]
        for i, r in enumerate(rs):
            lay[r] = (i, {"B": rs, "P": ranks[partner], "N": ranks[near], "O": ranks[other]})
    return lay


def peer(lay, r, w):
    i, chips = lay[r]
    return chips[w[0]][i if w[1] == "1" else 1 - i]


def relay_of(T, topo, lay, r):
    core = T.cores[r]
    return [k for k in topo.cores_of(core) if topo.die(k) != topo.die(core) and all(topo.may_write(k, d) for d in T.cores)][lay[r][0]]


def engine_sets(T, topo, lay, r):
    on = topo.engines(T.cores[r], T.cores[peer(lay, r, "B0")])
    off = topo.engines(T.cores[r], T.cores[peer(lay, r, "P0")])
    return on, off, [e for e in on if e not in off]


def engines_for(sets, rnd, w):
    on, off, inner = sets
    if w[2] == "d" and w[0] != "B":
        return off
    return on if len(rnd) == 1 else inner


def relay_program(g, core, T, topo):
    lay = layout(T, topo)
    m = T.sem
    for r in lay:
        if relay_of(T, topo, lay, r) != core:
            continue
        sets = engine_sets(T, topo, lay, r)
        a, b, arr = 256 * r, 256 * r + 256, m["arr%d" % r]
        to = T.cores[peer(lay, r, NAMES[5])]
        rid, pid, _ = topo.addr(to)
        eng = topo.engines(core, to)
        g.wait_ge(m.rl, len(sets[2]) // 2)
        g.remote_dma(T.ml[:, 10:12], T.rb[:], m.ml3, m.sent, pid, rid, bits(eng))
        for t in [t for t in ORDER_G if t[0] in "cp" and t[1:].isdigit()]:
            k = int(t[1])
            w = ROUNDS[k][0]
            if w[2] != "r":
                continue
            rid, pid, _ = topo.addr(T.cores[peer(lay, r, w)])
            g.wait_ge(m["r" + t], len(engines_for(sets, ROUNDS[k], w)))
            if t[0] == "c":
                g.remote_dma(T.lc[:, a:b].bitcast(U8), T.rlc[:, 256 * k:256 * k + 256].bitcast(U8), arr, m.sent, pid, rid, bits(eng))
            else:
                g.remote_dma(T.lp[:, a:b], T.rlp[:, 256 * k:256 * k + 256], arr, m.sent, pid, rid, bits(eng))
        g.wait_ge(m.sent, 7 * len(eng))


def rank_program(g, core, T, topo):
    rank = T.rank_of(core)
    if rank is None:
        return relay_program(g, core, T, topo)
    lay = layout(T, topo)
    i, chips = lay[rank]
    out = [peer(lay, rank, w) for w in NAMES]
    nbr, relay = out[6], relay_of(T, topo, lay, rank)
    sets = engine_sets(T, topo, lay, rank)
    on, off, inner = sets
    S, V, P, Y = g.scalar, g.vector, g.tensor, g.sync
    m = T.sem
    cnt = {"v": 0, "s": 0, "p": 0, "gq": 0, "sent": 0}
    seen = {}

    def did(ins, name):
        ins.then_inc(m[name], 1)
        cnt[name] += 1
        return cnt[name]

    def wait(queue, name, n):
        if seen.get((queue, name), 0) < n:
            seen[queue, name] = n
            {"v": V, "s": S, "p": P, "g": g, "y": Y}[queue].wait_ge(m[name], n)

    def v(ins): return did(ins, "v")
    def gq(ins): return did(ins, "gq")

    def dst_id(c):
        rid, pid, _ = topo.addr(c)
        return DstId(rid=rid, pnc=pid)

    def write(c, engines, sem, src, dst):
        cnt["sent"] += len(engines)
        return RemoteDMATransfer(dst_ids=[dst_id(c)], dma_engine_mask=bits(engines), remote_sem=m[sem], src=src, dst=dst)

    lo = min(rank, nbr)
    Y.dma_start(T.tv[0:1, :], T.tab[:]).then_inc(m.d_tab, 16)
    for k in range(4):
        (Y if k < 2 else S).dma_start(T.tokb[16 * k:16 * k + 16, :], T.tok[:]).then_inc(m.d_tok, 16)
    Y.dma_start(T.xsb[:], T.x[:]).then_inc(m.d_x, 16)
    for k in range(8):
        Y.dma_start(T.wab[:, 512 * k:512 * k + 512], T.wa[128 * k:128 * k + 128, :]).then_inc(m.d_wa, 16)

    gq(g.iota(T.ibp[:], [[0, 32]], 0, 1))
    g_a = gq(g.iota(T.ibc[:], [[16, 32]], 0, 0))
    gq(g.iota(T.ut[:], [[16, 16]], 64, 1))
    g_b = gq(g.iota(T.vals[:], [[1, 256]], 0, 16, allow_small_or_imprecise_dtypes=True))
    v(V.memset(T.inv[:, 0:1024], 0.0))
    wait("v", "gq", g_a)
    n = v(V.tensor_scalar(T.ibr[:], T.ibp[:], 15, None, AND))
    v(V.tensor_copy(T.pid[:], T.ibp[:, 0:2]))
    v(V.tensor_copy(T.pf[:], T.ibp[:, 0:2]))
    wait("v", "v", n)
    v_pre = v(V.tensor_tensor(T.base[:], T.ibr[:], T.ibc[:], ADD))

    outer = {"tab": ("gq", g_b + 1), "iota": ("gq", g_b), "d_tok": ("d_tok", 64), "e2": ("d_e2", 128), "nl": ("m_nl", len(inner) // 2)}
    small = {
        "Mb": (["tab"], lambda: V.tensor_scalar(T.mb[:], T.tb[:], 0, 512, MAX, MUL)),
        "Mi": (["tab"], lambda: V.tensor_scalar(T.mi[:], T.tb[:, 2 * lo:2 * lo + 4], 0, 128, MAX, MUL)),
        "Iu": (["Mi"], lambda: V.tensor_scalar(T.ixu[:], T.mi[:], T.pf[:, 0:1], None, ADD)),
        "Ix": (["Mi"], lambda: V.tensor_scalar(T.ix[:], T.mi[:], T.pf[:, 0:1], None, ADD)),
        "Jn": (["nl"], lambda: V.tensor_copy(T.ixn[:, 0:2], T.nu[:])),
        "tok": (["d_tok"], lambda: V.tensor_copy(T.tokb[64:128, :], T.tokb[0:64, :])),
        "Xo": (["tok"], lambda: V.tensor_scalar(T.xo[:], T.tokb[:], 0, 4, MAX, MUL)),
        "Tk": (["tok"], lambda: V.tensor_copy(T.tk2[:], T.tokb[:, 0:128].indirect(T.pid[:, 0:1]))),
        "Ka": (["Tk"], lambda: V.tensor_scalar(T.ka[:], T.tk2[:], 15, None, AND)),
        "Kb": (["Tk"], lambda: V.tensor_scalar(T.kb[:], T.tk2[:], 4, None, AluOpType.logical_shift_right)),
        "La": (["Ka"], lambda: V.tensor_scalar(T.ka2[:], T.ka[:], 64, None, MUL)),
        "Lb": (["Kb", "iota"], lambda: V.tensor_tensor(T.kb2[:], T.kb[:], T.ut[:], MIN)),
        "Kc": (["La", "Lb"], lambda: V.tensor_tensor(T.kc[:], T.ka2[:], T.kb2[:], ADD)),
        "So": (["Kc"], lambda: V.tensor_copy(T.so[:], T.kc[:])),
        "Inv": (["So"], lambda: V.tensor_copy(T.inv[:, 0:1392].indirect(T.so[:, 0:16]), T.vals[:])),
        "ad0": (["e2"], lambda: V.tensor_tensor(T.s1[:], T.mg[:, 0:256], T.mg[:, 256:512], ADD)),
        "ad1": (["ad0"], lambda: V.tensor_tensor(T.s2[:], T.s1[:, 0:128], T.s1[:, 128:256], ADD)),
        "ad2": (["ad1"], lambda: V.tensor_tensor(T.s3[:], T.s2[:, 0:64], T.s2[:, 64:128], ADD)),
        "ad3": (["ad2"], lambda: V.tensor_copy(T.yo[:], T.s3[:])),
    }

    arrive = [peer(lay, rank, w) for w in ("P1", "P0", "O1", "O0", "N1", "B0", "N0")]
    groups = [[2 * rank]] + [[2 * q, 2 * q + 1] for q in arrive[:PAIRS]]
    groups += [[sl] for q in arrive[PAIRS:] for sl in (2 * q, 2 * q + 1)] + [[2 * rank + 1]]
    ends = [sum(len(x) for x in groups[:k + 1]) for k in range(len(groups))]
    halves = [rank // 4, 1 - rank // 4]
    xchips = [chips[c] for c in "BPNO"]
    cols = [(256 * NAMES.index(rnd[0]), 256 * NAMES.index([w for w in rnd if w[0] != "B"][-1]) + 256) for rnd in ROUNDS]
    r0, r1 = 256 * rank, 256 * rank + 256

    todo = {"v": ORDER_V, "s": ORDER_S}
    done = {}
    for e in "vs":
        c = cnt[e]
        for t in todo[e]:
            c += (cols[int(t[1])][1] - cols[int(t[1])][0]) // 128 if t[0] == "o" else 1
            done[e, t] = c

    def need(queue, t):
        for e in "vs":
            if (e, t) in done:
                wait(queue, e, done[e, t])

    def move(e, dst, src):
        did(V.tensor_copy(dst, src) if e == "v" else S.activation(dst, src, COPY), e)

    def emit(e, t):
        if t in small:
            wait(e, "v", v_pre)
            for d in small[t][0]:
                if d in outer:
                    wait(e, *outer[d])
                need(e, d)
            v(small[t][1]())
        elif t[0] == "x":
            a, el = 64 * halves[int(t[1])], int(t[2])
            b = a + 64
            if len(t) > 3:
                a = 16 * xchips[2 * int(t[1]) + int(t[3])][0]
                b = a + 32
            need(e, "Xo")
            wait(e, "d_x", 16)
            move(e, T.hx[:, 64 * a + el:64 * b:4], T.xsb[:, el:4096].indirect(T.xo[:, a:b]))
        elif t[:2] == "qx":
            c = int(t[2])
            for el in range(4):
                need(e, "x%d%d" % (c // 2, el))
                need(e, "x%d%d%d" % (c // 2, el, c % 2))
            a = 256 * xchips[c][0]
            v(V.quantize_mx(T.xq[:, a:a + 512], T.xp[:, a:a + 512], T.hx[:, 4 * a:4 * a + 2048]))
        elif t[0] == "o":
            c0, c1 = cols[int(t[1])]
            for k in range(c0 // 128, c1 // 128):
                wait(e, "ml%d" % (3 if k >= 10 else k // 4), len(off))
                v(V.tensor_scalar(T.offu[:, 32 * k:32 * k + 32], T.base[:], T.ml[:, k:k + 1], None, ADD))
        elif t[0] == "a":
            c0, c1 = cols[int(t[1])]
            cut = 4 * c0 + (c1 - c0) // 4 * SHARE[int(t[1])]
            a, b = (4 * c0, cut) if e == "s" else (cut, 4 * c1)
            need(e, "o" + t[1])
            wait(e, "d_wa", 128)
            move(e, T.ga[:, a:b], T.wab[:, 0:4096].indirect(T.offu[:, a // 16:b // 16]))
        elif t[:2] == "qa":
            c0, c1 = cols[int(t[2])]
            need(e, t[1:])
            v(V.quantize_mx(T.aq[:, c0:c1], T.apl[:, c0:c1], T.ga[:, 4 * c0:4 * c1]))
        elif t == "qn":
            wait(e, "d_gn", 32)
            v(V.quantize_mx(T.aq[:, 1536:1792], T.apl[:, 1536:1792], T.gn[:]))
        elif t[:2] == "qo":
            k = int(t[2])
            a = r0 + 128 * k
            wait(e, "d_go%d" % k, 16)
            v(V.quantize_mx(T.lc[:, a:a + 128], T.lp[:, a:a + 128], T.go[:, 512 * k:512 * k + 512]))
        elif t[0] == "c":
            k = int(t[1:])
            a, n = 128 * groups[k][0], 128 * len(groups[k])
            wait(e, "p", ends[k])
            move(e, T.rsb[:, a:a + n], T.ps[:, 512 * (k % 8):512 * (k % 8) + n])
        else:
            a, b = Y_AT[int(t[1])], Y_AT[int(t[1]) + 1]
            need(e, "ad3")
            for k in range(len(groups)):
                need(e, "c%d" % k)
            move(e, T.ysb[:, a:b], T.rsb[:, 0:2048].indirect(T.yo[:, a // 16:b // 16]))

    for e in "vs":
        for t in todo[e]:
            emit(e, t)

    def rows(dst, ix, k, sem):
        g.indirect_dma_start(dst[:, 512 * k:512 * k + 512], None, T.wa[:], IndirectOffsetOnAxis(ap=ix, axis=0),
                             bounds_check=1023).then_inc(m[sem], 16)

    def entries(q):
        return T.mb[:, 2 * q:2 * q + 2]

    for t in ORDER_G:
        if t == "tab":
            wait("g", "d_tab", 16)
            gq(g.partition_broadcast(T.tb[:], T.tv[0:1, :], 128))
        elif t == "chip":
            need("g", "Iu")
            h = len(inner) // 2
            g.remote_dma_fused([write(T.cores[nbr], inner[:h], "m_nl", T.ixu[:, 2 - 2 * i:4 - 2 * i], T.nu[:]),
                                write(relay, inner[h:], "rl", entries(out[5]), T.rb[:])], local_sem=m.sent)
        elif t[0] == "l":
            need("g", "Mb")
            js = [j for j in (2 * int(t[1]), 2 * int(t[1]) + 1) if j < 5]
            h = len(off) // len(js)
            g.remote_dma_fused([write(T.cores[out[j]], off[h * (j % 2):h * (j % 2) + h], "m" + t, entries(out[j]), T.ml[:, 2 * j:2 * j + 2])
                                for j in js], local_sem=m.sent)
        elif t[:3] == "own":
            k = int(t[3])
            need("g", "Ix")
            rows(T.go, T.ix[:, 2 * i + k:2 * i + k + 1], k, "d_go%d" % k)
        elif t[:2] == "nb":
            k = int(t[2])
            need("g", "Jn")
            rows(T.gn, T.ixn[:, k:k + 1], k, "d_gn")
        else:
            k = int(t[1])
            need("g", "qa%d" % k)
            to = []
            for w in ROUNDS[k]:
                if w[0] == "B":
                    need("g", "qn")
                a = 256 * NAMES.index(w)
                if w[2] == "r":
                    c, sem, codes, planes = relay, "r" + t, T.rlc[:, 256 * k:256 * k + 256], T.rlp[:, 256 * k:256 * k + 256]
                else:
                    c, sem, codes, planes = T.cores[peer(lay, rank, w)], "arr%d" % rank, T.lc[:, r0:r1], T.lp[:, r0:r1]
                src, dst = (T.aq[:, a:a + 256].bitcast(U8), codes.bitcast(U8)) if t[0] == "c" else (T.apl[:, a:a + 256], planes)
                to.append(write(c, engines_for(sets, ROUNDS[k], w), sem, src, dst))
            g.remote_dma_fused(to, local_sem=m.sent)

    need("y", "Inv")
    for k in range(8):
        Y.dma_start(T.e2[:, k, :], T.inv[16 * k:16 * k + 1, 0:1024]).then_inc(m.d_e1, 16)
    wait("y", "d_e1", 128)
    for k in range(8):
        Y.dma_start(T.mg[16 * k:16 * k + 16, :], T.e2[:]).then_inc(m.d_e2, 16)
    for queue, q, k in (("y", Y, 0), ("y", Y, 2), ("y", Y, 1), ("s", S, 3)):
        need(queue, "y%d" % k)
        q.dma_start(T.y[:, Y_AT[k]:Y_AT[k + 1]], T.ysb[:, Y_AT[k]:Y_AT[k + 1]]).then_inc(m.d_y, 16)

    for k, grp in enumerate(groups):
        q = grp[0] // 2
        if q == rank:
            need("p", "qo%d" % (grp[0] % 2))
        else:
            wait("p", "arr%d" % q, 2 * len(inner if q == nbr else off))
        need("p", "qx%d" % [q in c for c in xchips].index(True))
        if k >= 8:
            need("p", "c%d" % (k - 8))
        a = 128 * grp[0]
        for sl in reversed(grp):
            w, b = 128 * sl, 128 * sl + 128
            if sl != grp[-1]:
                wait("p", "p", cnt["p"])
            did(P.matmul_mx(T.ps[:, 512 * (k % 8):512 * (k % 8) + b - a], T.lc[:, w:b], T.lp[:, w:b], T.xq[:, a:b], T.xp[:, a:b],
                            True, True), "p")

    g.wait_ge(m.sent, cnt["sent"])
    g.wait_ge(m.d_y, 64)
    for name in ("v", "s", "p", "gq"):
        g.wait_ge(m[name], cnt[name])
